import numpy as np
import ml_dtypes


def mxq(x, axis, fmt="e4m3"):
    dtype, down = {"e4m3": (ml_dtypes.float8_e4m3fn, 7), "e5m2": (ml_dtypes.float8_e5m2, 14)}[fmt]
    v = np.moveaxis(np.asarray(x, np.float32).astype(ml_dtypes.bfloat16).astype(np.float64), axis, -1)
    blocks = v.reshape(v.shape[:-1] + (-1, 32))
    amax = np.abs(blocks).max(-1, keepdims=True)
    byte = np.maximum(np.where(amax > 0, np.frexp(amax)[1] - 1 + 127, 0) - down, 1)
    scale = np.exp2(byte - 127.0)
    codes = (blocks / scale).astype(np.float32).astype(dtype).astype(np.float64)
    return np.moveaxis((codes * scale).reshape(v.shape), -1, axis)


WIDE = False


def mx_kscale(k):
    if not WIDE:
        return np.ones(k)
    levels = np.array([10, -10, 5, -5, 0])
    if k % 512:
        return np.exp2(np.random.permutation(np.resize(levels, k // 32))).repeat(32)
    a = np.empty((k // 512, 16))
    for p in range(k // 512):
        a[p, :8] = np.random.permutation(np.resize(levels, 8))
        for g in range(8):
            far = levels[np.abs(levels - a[p, g]) >= 10]
            a[p, g + 8] = far[np.random.randint(len(far))]
    return np.exp2(a.ravel()).repeat(32)


def f64(x):
    return np.asarray(x).astype(np.float64)


def striped(idx):
    return np.tile(idx.reshape(-1, 16).T, (8, 1)).astype(np.uint16)


def unstriped(offs):
    return offs[:16].T.reshape(-1).astype(np.int64)


def striped8(idx):
    return np.concatenate([x.reshape(-1, 16).T for x in idx]).astype(np.uint16)


def runs(offs, k):
    lists = np.stack([offs[16 * r : 16 * r + 16].T.reshape(-1) for r in range(8)]).astype(np.int64)
    return lists[np.arange(k) % 512 // 64]


def pack_weight(w):
    k, n = w.shape
    w = f64(np.asarray(w, np.float32).astype(ml_dtypes.bfloat16)).reshape(k // 32, 32, n)
    amax = np.abs(w).max(1)
    byte = np.clip(np.where(amax > 0, np.frexp(amax)[1] - 1 + 127 - 7, 1), 1, 254)
    scaled = (w * np.exp2(127.0 - byte)[:, None, :]).reshape(k, n).astype(np.float32)
    words = np.ascontiguousarray(scaled.reshape(k // 512, 128, 4, n).transpose(0, 1, 3, 2)).astype(ml_dtypes.float8_e4m3fn).view(np.uint8)
    return words, np.ascontiguousarray(byte.astype(np.uint8).reshape(k // 512, 16, n))


def unpack_weight(words, scales):
    g, p, n, _ = words.shape
    vals = np.ascontiguousarray(words).view(ml_dtypes.float8_e4m3fn).astype(np.float64) * np.repeat(np.exp2(scales.astype(np.float64) - 127.0), 8, axis=1)[..., None]
    return vals.transpose(0, 1, 3, 2).reshape(g * 512, n)


E2M1 = np.array([0.0, 0.5, 1.0, 1.5, 2.0, 3.0, 4.0, 6.0, -0.0, -0.5, -1.0, -1.5, -2.0, -3.0, -4.0, -6.0])


def pack_fp4(w):
    k, n = w.shape
    w = f64(np.asarray(w, np.float32).astype(ml_dtypes.bfloat16)).reshape(k // 32, 32, n)
    amax = np.abs(w).max(1)
    mant, ex = np.frexp(amax / 6.0)
    byte = np.clip(np.where(amax > 0, np.where(mant > 0.5, ex, ex - 1) + 127, 1), 1, 254)
    scaled = (w * np.exp2(127.0 - byte)[:, None, :]).reshape(k, n).astype(np.float32)
    c = np.ascontiguousarray(scaled.reshape(k // 512, 128, 4, n).transpose(0, 1, 3, 2)).astype(ml_dtypes.float4_e2m1fn).view(np.uint8) & 0xF
    words = (c[..., 0::2] | (c[..., 1::2] << 4)).reshape(k // 512, 128, 2 * n)
    return np.ascontiguousarray(words), np.ascontiguousarray(byte.astype(np.uint8).reshape(k // 512, 16, n))


def unpack_fp4(words, scales):
    g, _, n = scales.shape
    words = np.ascontiguousarray(words).reshape(g, 128, n, 2)
    nib = np.empty((g, 128, n, 4), np.uint8)
    nib[..., 0::2] = words & 0xF
    nib[..., 1::2] = words >> 4
    vals = E2M1[nib] * np.repeat(np.exp2(scales.astype(np.float64) - 127.0), 8, axis=1)[..., None]
    return vals.transpose(0, 1, 3, 2).reshape(g * 512, n)


def planes(y):
    n, m = y.shape
    v = y.astype(np.float32).astype(ml_dtypes.bfloat16).astype(np.float64).reshape(n // 32, 32, m)
    top = np.abs(v).max(1)
    byte = np.clip(np.where(top > 0, np.frexp(top)[1] - 1 + 127 - 7, 1), 1, 254)
    codes = (v * np.exp2(127.0 - byte)[:, None, :]).reshape(n, m).astype(np.float32).astype(ml_dtypes.float8_e4m3fn).view(np.uint8)
    words = codes.reshape(n // 512, 128, 4, m).transpose(0, 1, 3, 2)
    return np.ascontiguousarray(words), np.ascontiguousarray(byte.astype(np.uint8).reshape(n // 512, 16, m))


K, T, S, N, H, G, W = 512, 2048, 512, 512, 512, 2048, 256


def setup_inputs():
    n = np.random.standard_normal
    s = mx_kscale(K)[:, None]
    u = mx_kscale(S)
    packed_xT = pack_weight(n((K, T)) * s)
    packed_w1 = pack_fp4(n((K, H)) / np.sqrt(K) / s)
    packed_dT = pack_weight(n((K, G)) / s)
    packed_w2 = pack_fp4(n((H, N)) / np.sqrt(H) / u[:, None])
    perm = np.random.permutation(S)
    return {
        "x_words": packed_xT[0],
        "x_scales": packed_xT[1],
        "w1_words": packed_w1[0],
        "w1_scales": packed_w1[1],
        "d_words": packed_dT[0],
        "d_scales": packed_dT[1],
        "gn": (np.random.uniform(0.5, 1.5, (H, 1)) * u[:, None]).astype(np.float32),
        "w2_words": packed_w2[0],
        "w2_scales": packed_w2[1],
        "offs": striped(np.random.permutation(T)[:S]),
        "k1": striped8(np.random.randint(0, G, (8, H))),
        "two": striped(np.random.permutation(T)[:S]),
        "n1": striped(np.random.permutation(S)),
        "n2": striped(np.random.permutation(S)),
        "n3": striped(np.random.permutation(S)),
        "n4": striped(perm[:W]),
        "n5": striped(perm[W:]),
    }


def reference(x_words, x_scales, w1_words, w1_scales, d_words, d_scales, gn, w2_words, w2_scales, offs, k1, two, n1, n2, n3, n4, n5):
    d_k1 = unpack_weight(d_words, d_scales)[np.arange(K)[:, None], runs(k1, K)]
    x_two = unpack_weight(x_words, x_scales)[:, unstriped(two)]
    d = 0.0625 * (d_k1.T @ x_two)
    xq = unpack_weight(x_words, x_scales)[:, unstriped(offs)]
    y = unpack_fp4(w1_words, w1_scales).T @ xq
    z = f64(gn) * (d * (y[:, unstriped(n1)] - y) + 0.5 * (d[:, unstriped(n3)] * (y[:, unstriped(n2)] - y)))
    h = unpack_fp4(w2_words, w2_scales).T @ mxq(z, 0, "e4m3")
    pa = h[:, unstriped(n4)]
    pb = h[:, unstriped(n5)]
    rb = np.maximum(pa, pb)
    ra = pa / (np.abs(pb) + 0.5)
    ds = np.zeros((N, S))
    ds[:, unstriped(n4)] = ra
    out = ds.copy()
    out[:, unstriped(n5)] = rb
    return (out,) + planes(out)

@@ -1,0 +1,272 @@
+from contextlib import ExitStack
+
+import concourse.mybir as mybir
+
+F32 = mybir.dt.float32
+BF16 = mybir.dt.bfloat16
+I32 = mybir.dt.int32
+U32 = mybir.dt.uint32
+U16 = mybir.dt.uint16
+U8 = mybir.dt.uint8
+FP8X4 = mybir.dt.float8_e4m3fn_x4
+FP4X4 = mybir.dt.float4_e2m1fn_x4
+ALU = mybir.AluOpType
+ACT = mybir.ActivationFunctionType
+
+P = 128
+PACK = 4
+S = 512
+T = 2048
+W = 256
+HALF = 256
+FLOPS = 3 * 2 * 512 * 512 * 512
+
+
+def tile_picked_twkeyflowbratio_none_po_kernel(
+    tc, x_words, x_scales, w1_words, w1_scales, d_words, d_scales, gn, w2_words, w2_scales,
+    offs, k1, two, n1, n2, n3, n4, n5, out_0, out_1, out_2,
+):
+    nc = tc.nc
+    with ExitStack() as ctx:
+        lists = ctx.enter_context(tc.tile_pool(name="lists", bufs=1))
+        sb = ctx.enter_context(tc.tile_pool(name="sb", bufs=1))
+        psum = ctx.enter_context(tc.psum_pool(name="psum", bufs=1))
+
+        def tile(shape, dtype, name):
+            return sb.tile(shape, dtype, name=name, align_bytes=64)
+
+        def load_list(src, name):
+            t = lists.tile(list(src.shape), U16, name=name)
+            nc.sync.dma_start(t[:], src)
+            return t
+
+        def load_scales(queue, dst, src):
+            for q in range(4):
+                queue.dma_start(dst[32 * q : 32 * q + 4, :].bitcast(I32), src[0, 4 * q : 4 * q + 4, :].bitcast(I32))
+
+        xs_win = tile([P, T], U8, "xs_win")
+        ds_win = tile([P, T], U8, "ds_win")
+        w1s_raw = tile([P, S], U8, "w1s_raw")
+        w2s_raw = tile([P, S], U8, "w2s_raw")
+        nc.vector.memset(xs_win[:, : 3 * T // 4].bitcast(I32), 0)
+        nc.gpsimd.memset(xs_win[:, 3 * T // 4 :].bitcast(I32), 0)
+        nc.gpsimd.memset(w1s_raw[:].bitcast(I32), 0)
+        nc.vector.memset(ds_win[:].bitcast(I32), 0)
+        nc.gpsimd.memset(w2s_raw[:].bitcast(I32), 0)
+
+        xw_win = tile([P, T], U32, "xw_win")
+        dw_win = tile([P, T], U32, "dw_win")
+        w1w_raw = tile([P, 2 * S], U8, "w1w_raw")
+        w2w_raw = tile([P, 2 * S], U8, "w2w_raw")
+        gn_sb = tile([P, PACK], F32, "gn_sb")
+
+        load_scales(nc.sync, xs_win, x_scales)
+        offs_t = load_list(offs, "offs_t")
+        two_t = load_list(two, "two_t")
+        nc.sync.dma_start(w1w_raw[:].bitcast(I32), w1_words[0].bitcast(I32))
+        nc.sync.dma_start(xw_win[:].bitcast(I32), x_words[0].rearrange("p n r -> p (n r)").bitcast(I32))
+        load_scales(nc.sync, w1s_raw, w1_scales)
+        k1_t = load_list(k1, "k1_t")
+        for e in range(2):
+            nc.sync.dma_start(ds_win[e:P:16, :].bitcast(I32), d_scales[0, e:16:2, :].bitcast(I32))
+        nc.sync.dma_start(dw_win[:].bitcast(I32), d_words[0].rearrange("p n r -> p (n r)").bitcast(I32))
+        n1_t = load_list(n1, "n1_t")
+        n2_t = load_list(n2, "n2_t")
+        nc.sync.dma_start(w2w_raw[:].bitcast(I32), w2_words[0].bitcast(I32))
+        load_scales(nc.sync, w2s_raw, w2_scales)
+        nc.sync.dma_start(gn_sb[:], gn.rearrange("(p t) o -> p (t o)", t=PACK))
+        n3_t = load_list(n3, "n3_t")
+        n4_t = load_list(n4, "n4_t")
+        n5_t = load_list(n5, "n5_t")
+
+        def deal_weight(engine, words_raw, scales_raw, name):
+            words = tile([P, 2 * S], U8, name + "w")
+            scales = tile([P, S], U8, name + "s")
+            engine.tensor_copy(
+                words[:].rearrange("p (t m b) -> p t m b", t=PACK, b=2),
+                words_raw[:].rearrange("p (m t b) -> p t m b", t=PACK, b=2),
+            )
+            engine.tensor_copy(
+                scales[:].rearrange("p (t m) -> p t m", t=PACK),
+                scales_raw[:].rearrange("p (m t) -> p t m", t=PACK),
+            )
+            return words, scales
+
+        xq_s = tile([P, S], U8, "xq_s")
+        xq_w = tile([P, S], U32, "xq_w")
+        x2_s = tile([P, S], U8, "x2_s")
+        x2_w = tile([P, S], U32, "x2_w")
+        dk_s_raw = tile([P, S], U8, "dk_s_raw")
+        dk_w_raw = tile([P, S], U32, "dk_w_raw")
+        dk_s = tile([P, S], U8, "dk_s")
+        dk_w = tile([P, S], U32, "dk_w")
+
+        nc.vector.tensor_copy(xq_s[:], xs_win[:].indirect(offs_t[:]))
+        w1w, w1s = deal_weight(nc.vector, w1w_raw, w1s_raw, "w1")
+        nc.vector.tensor_copy(xq_w[:], xw_win[:].indirect(offs_t[:]))
+
+        y_ps = []
+        for t in range(PACK):
+            bank = psum.tile([P, S], F32, name="y_ps%d" % t, tag="bank_a%d" % t)
+            nc.tensor.matmul_mx(
+                bank[:], lhsT=w1w[:, 2 * P * t : 2 * P * (t + 1)].bitcast(FP4X4), lhsT_scale=w1s[:, P * t : P * (t + 1)],
+                rhs=xq_w[:].bitcast(FP8X4), rhs_scale=xq_s[:], start=True, stop=True,
+            )
+            y_ps.append(bank)
+
+        nc.vector.tensor_copy(dk_s_raw[:], ds_win[:].indirect(k1_t[:]))
+        nc.vector.tensor_copy(
+            dk_s[:].rearrange("p (t m) -> p t m", t=PACK), dk_s_raw[:].rearrange("p (m t) -> p t m", t=PACK)
+        )
+        for e in range(2):
+            nc.sync.dma_start(dk_s[2 + e : P : 32, :].bitcast(I32), dk_s[16 + e : P : 32, :].bitcast(I32))
+        nc.vector.tensor_copy(x2_s[:], xs_win[:].indirect(two_t[:]))
+        nc.vector.tensor_copy(x2_w[:], xw_win[:].indirect(two_t[:]))
+        nc.vector.tensor_copy(dk_w_raw[:], dw_win[:].indirect(k1_t[:]))
+        nc.vector.tensor_copy(
+            dk_w[:].rearrange("p (t m) -> p t m", t=PACK), dk_w_raw[:].rearrange("p (m t) -> p t m", t=PACK)
+        )
+        d_ps = []
+        for t in range(PACK):
+            bank = psum.tile([P, S], F32, name="d_ps%d" % t, tag="bank_b%d" % t)
+            nc.tensor.matmul_mx(
+                bank[:], lhsT=dk_w[:, P * t : P * (t + 1)].bitcast(FP8X4), lhsT_scale=dk_s[:, P * t : P * (t + 1)],
+                rhs=x2_w[:].bitcast(FP8X4), rhs_scale=x2_s[:], start=True, stop=True,
+            )
+            d_ps.append(bank)
+
+        gain = tile([P, PACK], F32, "gain")
+        nc.gpsimd.tensor_scalar(gain[:], gn_sb[:], 1.0 / 32.0, 0.0, ALU.mult, ALU.add)
+        w2w, w2s = deal_weight(nc.gpsimd, w2w_raw, w2s_raw, "w2")
+
+        y_sb = [tile([P, S], F32, "y_sb%d" % t) for t in range(PACK)]
+        d_sb = [tile([P, S], F32, "d_sb%d" % t) for t in range(PACK)]
+        h_sb = [tile([P, S], F32, "h_sb%d" % t) for t in range(PACK)]
+        LC = HALF // 16
+
+        picked = [[tile([P, 2, HALF], F32, "picked%d_%d" % (u, t)) for t in range(PACK)] for u in range(2)]
+        for t in range(PACK):
+            nc.scalar.activation(y_sb[t][:], y_ps[t][:], ACT.Copy)
+            nc.scalar.activation(picked[0][t][:, 0, :], y_sb[t][:].indirect(n1_t[:, 0:LC]), ACT.Copy)
+            nc.scalar.activation(picked[0][t][:, 1, :], y_sb[t][:].indirect(n2_t[:, 0:LC]), ACT.Copy)
+        for t in range(PACK):
+            nc.scalar.activation(d_sb[t][:], d_ps[t][:], ACT.Copy, scale=gain[:, t : t + 1])
+        d_far = [tile([P, HALF], F32, "d_far%d" % t) for t in range(PACK)]
+        for t in range(PACK):
+            nc.scalar.activation(picked[1][t][:, 0, :], y_sb[t][:].indirect(n1_t[:, LC : 2 * LC]), ACT.Copy)
+            nc.scalar.activation(picked[1][t][:, 1, :], y_sb[t][:].indirect(n2_t[:, LC : 2 * LC]), ACT.Copy)
+            nc.scalar.activation(d_far[t][:], d_sb[t][:].indirect(n3_t[:, LC : 2 * LC]), ACT.Copy)
+
+        h_ps = [[], []]
+        for u in range(2):
+            cols = slice(u * HALF, (u + 1) * HALF)
+            near = tile([P, PACK, HALF], F32, "near%d" % u)
+            far = tile([P, PACK, HALF], F32, "far%d" % u)
+            diff = [tile([P, 2, HALF], F32, "diff%d_%d" % (u, t)) for t in range(PACK)]
+
+            def differences(t):
+                nc.vector.tensor_tensor(
+                    diff[t][:], picked[u][t][:], y_ps[t][:, cols].unsqueeze(1).to_broadcast([P, 2, HALF]), ALU.subtract
+                )
+
+            def products(t):
+                nc.vector.scalar_tensor_tensor(near[:, t, :], diff[t][:, 0, :], 2.0, d_sb[t][:, cols], ALU.mult, ALU.mult)
+                if u == 0:
+                    nc.vector.tensor_tensor(far[:, t, :], d_sb[t][:].indirect(n3_t[:, 0:LC]), diff[t][:, 1, :], ALU.mult)
+                else:
+                    nc.vector.tensor_tensor(far[:, t, :], d_far[t][:], diff[t][:, 1, :], ALU.mult)
+
+            if u == 0:
+                for t in range(PACK):
+                    differences(t)
+                for t in range(PACK):
+                    products(t)
+            else:
+                differences(0)
+                for t in range(PACK):
+                    if t + 1 < PACK:
+                        differences(t + 1)
+                    products(t)
+            z_bf = tile([P, HALF * PACK], BF16, "z_bf%d" % u)
+            nc.vector.tensor_tensor(
+                z_bf[:].rearrange("p (c i t) -> p c t i", i=4, t=PACK),
+                near[:].rearrange("p t (c i) -> p c t i", i=4),
+                far[:].rearrange("p t (c i) -> p c t i", i=4),
+                ALU.add,
+            )
+            z_w = tile([P, HALF], U32, "z_w%d" % u)
+            z_s = tile([P, HALF], U8, "z_s%d" % u)
+            nc.vector.quantize_mx(z_w[:].bitcast(FP8X4), z_s[:], z_bf[:])
+            for t in range(PACK):
+                bank = psum.tile([P, HALF], F32, name="h_ps%d_%d" % (u, t), tag=("bank_b%d" if u == 0 else "bank_a%d") % t)
+                nc.tensor.matmul_mx(
+                    bank[:], lhsT=w2w[:, 2 * P * t : 2 * P * (t + 1)].bitcast(FP4X4), lhsT_scale=w2s[:, P * t : P * (t + 1)],
+                    rhs=z_w[:].bitcast(FP8X4), rhs_scale=z_s[:], start=True, stop=True,
+                )
+                h_ps[u].append(bank)
+                if u == 0:
+                    nc.scalar.activation(h_sb[t][:, cols], bank[:], ACT.Copy)
+
+        out_rows = out_0.rearrange("(p t) j -> p t j", t=PACK)
+        pa = [tile([P, W], F32, "pa%d" % t) for t in range(PACK)]
+        pb = [tile([P, W], F32, "pb%d" % t) for t in range(PACK)]
+        size = [tile([P, W], F32, "size%d" % t) for t in range(PACK)]
+        root = [tile([P, W], F32, "root%d" % t) for t in range(PACK)]
+        larger = [tile([P, W], F32, "larger%d" % t) for t in range(PACK)]
+        part = [tile([P, W], F32, "part%d" % t) for t in range(PACK)]
+        o_sb = [tile([P, S], F32, "o_sb%d" % t) for t in range(PACK)]
+        o_pl = tile([P, PACK, S], BF16, "o_pl")
+        o_bf = tile([P, S * PACK], BF16, "o_bf")
+
+        def fetch(t):
+            if t == 2:
+                nc.vector.tensor_copy(h_sb[t][:, HALF:], h_ps[1][t][:])
+            else:
+                nc.scalar.activation(h_sb[t][:, HALF:], h_ps[1][t][:], ACT.Copy)
+            nc.scalar.activation(pa[t][:], h_sb[t][:].indirect(n4_t[:]), ACT.Copy)
+            nc.vector.tensor_copy(pb[t][:], h_sb[t][:].indirect(n5_t[:]))
+
+        def combine(t):
+            nc.vector.scalar_tensor_tensor(size[t][:], pb[t][:], -1.0, pb[t][:], ALU.mult, ALU.max)
+            nc.vector.tensor_tensor(larger[t][:], pa[t][:], pb[t][:], ALU.max)
+
+        def put_larger(t):
+            nc.scalar.activation(root[t][:], size[t][:], ACT.Abs_reciprocal_sqrt, bias=0.5)
+            nc.scalar.activation(o_sb[t][:].indirect(n5_t[:]), larger[t][:], ACT.Copy)
+            nc.vector.tensor_tensor(part[t][:], pa[t][:], root[t][:], ALU.mult)
+
+        def put_ratio(t):
+            nc.vector.tensor_tensor(o_sb[t][:].indirect(n4_t[:]), part[t][:], root[t][:], ALU.mult)
+            nc.sync.dma_start(out_rows[:, t, :], o_sb[t][:])
+
+        fetch(0)
+        combine(0)
+        fetch(1)
+        combine(1)
+        put_larger(0)
+        fetch(2)
+        put_ratio(0)
+        combine(2)
+        put_larger(1)
+        put_ratio(1)
+        fetch(3)
+        combine(3)
+        put_larger(2)
+        put_ratio(2)
+        put_larger(3)
+        put_ratio(3)
+        for t in range(PACK - 1):
+            nc.scalar.activation(o_pl[:, t, :], o_sb[t][:], ACT.Copy)
+        nc.vector.tensor_copy(o_pl[:, PACK - 1, :], o_sb[PACK - 1][:])
+        CUT = 352 // 4
+        woven = o_bf[:].rearrange("p (c i t) -> p c t i", i=4, t=PACK)
+        planes = o_pl[:].rearrange("p t (c i) -> p c t i", i=4)
+        nc.vector.tensor_copy(woven[:, :CUT], planes[:, :CUT])
+        nc.scalar.copy(woven[:, CUT:], planes[:, CUT:])
+
+        o_w = tile([P, S], U32, "o_w")
+        o_s = tile([P, S], U8, "o_s")
+        nc.vector.quantize_mx(o_w[:].bitcast(FP8X4), o_s[:], o_bf[:])
+        nc.sync.dma_start(out_1[0].rearrange("p n r -> p (n r)").bitcast(I32), o_w[:].bitcast(I32))
+        for q in range(4):
+            nc.scalar.dma_start(out_2[0, 4 * q : 4 * q + 4, :].bitcast(I32), o_s[32 * q : 32 * q + 4, :].bitcast(I32))

@@ -32,8 +32,13 @@ def tile_picked_twkeyflowbratio_none_po_kernel(
         sb = ctx.enter_context(tc.tile_pool(name="sb", bufs=1))
         psum = ctx.enter_context(tc.psum_pool(name="psum", bufs=1))
 
-        def tile(shape, dtype, name):
-            return sb.tile(shape, dtype, name=name, align_bytes=64)
+        turn = ctx.enter_context(tc.tile_pool(name="turn", bufs=1))
+
+        def tile(shape, dtype, name, tag=""):
+            return sb.tile(shape, dtype, name=name, tag=tag, align_bytes=64)
+
+        def placed(shape, dtype, name, offset):
+            return turn.tile(shape, dtype, name=name, offset=offset, align_bytes=64)
 
         def load_list(src, name):
             t = lists.tile(list(src.shape), U16, name=name)
@@ -46,7 +51,7 @@ def tile_picked_twkeyflowbratio_none_po_kernel(
 
         xs_win = tile([P, T], U8, "xs_win")
         ds_win = tile([P, T], U8, "ds_win")
-        w1s_raw = tile([P, S], U8, "w1s_raw")
+        w1s_raw = tile([P, S], U8, "w1s_raw", "dealt_d_scales")
         w2s_raw = tile([P, S], U8, "w2s_raw")
         nc.vector.memset(xs_win[:, : 3 * T // 4].bitcast(I32), 0)
         nc.gpsimd.memset(xs_win[:, 3 * T // 4 :].bitcast(I32), 0)
@@ -54,33 +59,35 @@ def tile_picked_twkeyflowbratio_none_po_kernel(
         nc.vector.memset(ds_win[:].bitcast(I32), 0)
         nc.gpsimd.memset(w2s_raw[:].bitcast(I32), 0)
 
+        warm = tile([P, 2], F32, "warm")
+        nc.vector.memset(warm[:, 0:1], 1.0)
+        nc.scalar.activation(warm[:, 1:2], warm[:, 0:1], ACT.Abs_reciprocal_sqrt)
         xw_win = tile([P, T], U32, "xw_win")
         dw_win = tile([P, T], U32, "dw_win")
         w1w_raw = tile([P, 2 * S], U8, "w1w_raw")
         w2w_raw = tile([P, 2 * S], U8, "w2w_raw")
-        gn_sb = tile([P, PACK], F32, "gn_sb")
+        gn_wide = placed([P, 32], F32, "gn_wide", 16384 - 64)
+        gn_sb = gn_wide[:, 0:PACK]
 
         load_scales(nc.sync, xs_win, x_scales)
         offs_t = load_list(offs, "offs_t")
         two_t = load_list(two, "two_t")
         nc.sync.dma_start(w1w_raw[:].bitcast(I32), w1_words[0].bitcast(I32))
+        k1_t = load_list(k1, "k1_t")
+        nc.sync.dma_start(ds_win[0:P:8, :].bitcast(I32), d_scales[0].bitcast(I32))
         nc.sync.dma_start(xw_win[:].bitcast(I32), x_words[0].rearrange("p n r -> p (n r)").bitcast(I32))
         load_scales(nc.sync, w1s_raw, w1_scales)
-        k1_t = load_list(k1, "k1_t")
-        for e in range(2):
-            nc.sync.dma_start(ds_win[e:P:16, :].bitcast(I32), d_scales[0, e:16:2, :].bitcast(I32))
         nc.sync.dma_start(dw_win[:].bitcast(I32), d_words[0].rearrange("p n r -> p (n r)").bitcast(I32))
         n1_t = load_list(n1, "n1_t")
         n2_t = load_list(n2, "n2_t")
+        nc.sync.dma_start(gn_sb, gn.rearrange("(p t) o -> p (t o)", t=PACK))
+        n3_t = load_list(n3, "n3_t")
         nc.sync.dma_start(w2w_raw[:].bitcast(I32), w2_words[0].bitcast(I32))
         load_scales(nc.sync, w2s_raw, w2_scales)
-        nc.sync.dma_start(gn_sb[:], gn.rearrange("(p t) o -> p (t o)", t=PACK))
-        n3_t = load_list(n3, "n3_t")
         n4_t = load_list(n4, "n4_t")
         n5_t = load_list(n5, "n5_t")
 
-        def deal_weight(engine, words_raw, scales_raw, name):
-            words = tile([P, 2 * S], U8, name + "w")
+        def deal_weight(engine, words, words_raw, scales_raw, name):
             scales = tile([P, S], U8, name + "s")
             engine.tensor_copy(
                 words[:].rearrange("p (t m b) -> p t m b", t=PACK, b=2),
@@ -95,14 +102,23 @@ def tile_picked_twkeyflowbratio_none_po_kernel(
         xq_s = tile([P, S], U8, "xq_s")
         xq_w = tile([P, S], U32, "xq_w")
         x2_s = tile([P, S], U8, "x2_s")
-        x2_w = tile([P, S], U32, "x2_w")
-        dk_s_raw = tile([P, S], U8, "dk_s_raw")
-        dk_w_raw = tile([P, S], U32, "dk_w_raw")
+        dk_s_raw = tile([P, S], U8, "dk_s_raw", "after_d_scales")
+        x2_w = tile([P, S], U32, "x2_w", "after_d_scales")
+        dk_w_raw = placed([P, S], U32, "dk_w_raw", 2 * S)
+        dk_s_dealt = tile([P, S], U8, "dk_s_dealt", "dealt_d_scales")
         dk_s = tile([P, S], U8, "dk_s")
+        nc.gpsimd.memset(dk_s[:].bitcast(I32), 0)
         dk_w = tile([P, S], U32, "dk_w")
 
         nc.vector.tensor_copy(xq_s[:], xs_win[:].indirect(offs_t[:]))
-        w1w, w1s = deal_weight(nc.vector, w1w_raw, w1s_raw, "w1")
+        w1w, w1s = deal_weight(nc.gpsimd, tile([P, 2 * S], U8, "w1w"), w1w_raw, w1s_raw, "w1")
+        nc.vector.tensor_copy(x2_s[:], xs_win[:].indirect(two_t[:]))
+        nc.vector.tensor_copy(dk_s_raw[:], ds_win[:].indirect(k1_t[:]))
+        nc.vector.tensor_copy(
+            dk_s_dealt[:].rearrange("p (t m) -> p t m", t=PACK), dk_s_raw[:].rearrange("p (m t) -> p t m", t=PACK)
+        )
+        for q in range(4):
+            nc.sync.dma_start(dk_s[32 * q : 32 * q + 4, :].bitcast(I32), dk_s_dealt[32 * q : 32 * q + 32 : 8, :].bitcast(I32))
         nc.vector.tensor_copy(xq_w[:], xw_win[:].indirect(offs_t[:]))
 
         y_ps = []
@@ -114,13 +130,6 @@ def tile_picked_twkeyflowbratio_none_po_kernel(
             )
             y_ps.append(bank)
 
-        nc.vector.tensor_copy(dk_s_raw[:], ds_win[:].indirect(k1_t[:]))
-        nc.vector.tensor_copy(
-            dk_s[:].rearrange("p (t m) -> p t m", t=PACK), dk_s_raw[:].rearrange("p (m t) -> p t m", t=PACK)
-        )
-        for e in range(2):
-            nc.sync.dma_start(dk_s[2 + e : P : 32, :].bitcast(I32), dk_s[16 + e : P : 32, :].bitcast(I32))
-        nc.vector.tensor_copy(x2_s[:], xs_win[:].indirect(two_t[:]))
         nc.vector.tensor_copy(x2_w[:], xw_win[:].indirect(two_t[:]))
         nc.vector.tensor_copy(dk_w_raw[:], dw_win[:].indirect(k1_t[:]))
         nc.vector.tensor_copy(
@@ -135,58 +144,83 @@ def tile_picked_twkeyflowbratio_none_po_kernel(
             )
             d_ps.append(bank)
 
-        gain = tile([P, PACK], F32, "gain")
-        nc.gpsimd.tensor_scalar(gain[:], gn_sb[:], 1.0 / 32.0, 0.0, ALU.mult, ALU.add)
-        w2w, w2s = deal_weight(nc.gpsimd, w2w_raw, w2s_raw, "w2")
+        w2w, w2s = deal_weight(nc.gpsimd, placed([P, 2 * S], U8, "w2w", 4 * S), w2w_raw, w2s_raw, "w2")
 
         y_sb = [tile([P, S], F32, "y_sb%d" % t) for t in range(PACK)]
         d_sb = [tile([P, S], F32, "d_sb%d" % t) for t in range(PACK)]
         h_sb = [tile([P, S], F32, "h_sb%d" % t) for t in range(PACK)]
         LC = HALF // 16
 
-        picked = [[tile([P, 2, HALF], F32, "picked%d_%d" % (u, t)) for t in range(PACK)] for u in range(2)]
+        def on_scalar(u, t):
+            return u == 1
+
+        picked = [tile([P, PACK, 3, HALF], F32, "picked0"), placed([P, PACK, 3, HALF], F32, "picked1", 16384)]
+
+        def road(u, t):
+            return "F" if u == 0 and t < 2 else "S"
+
+        def leave_d(t):
+            if True:
+                nc.vector.tensor_scalar(d_sb[t][:], d_ps[t][:], gn_sb[:, t : t + 1], None, ALU.mult)
+            else:
+                nc.scalar.activation(d_sb[t][:], d_ps[t][:], ACT.Copy, scale=gn_sb[:, t : t + 1])
+
+        def fetch_y(u, t):
+            nc.scalar.activation(picked[u][:, t, 0, :], y_sb[t][:].indirect(n1_t[:, u * LC : (u + 1) * LC]), ACT.Copy)
+            nc.scalar.activation(picked[u][:, t, 1, :], y_sb[t][:].indirect(n2_t[:, u * LC : (u + 1) * LC]), ACT.Copy)
+
+        def fetch_d(u, t):
+            window = d_sb[t][:].indirect(n3_t[:, u * LC : (u + 1) * LC])
+            if road(u, t) == "S":
+                nc.scalar.activation(picked[u][:, t, 2, :], window, ACT.Copy)
+            if road(u, t) == "V":
+                nc.vector.tensor_copy(picked[u][:, t, 2, :], window)
+
         for t in range(PACK):
-            nc.scalar.activation(y_sb[t][:], y_ps[t][:], ACT.Copy)
-            nc.scalar.activation(picked[0][t][:, 0, :], y_sb[t][:].indirect(n1_t[:, 0:LC]), ACT.Copy)
-            nc.scalar.activation(picked[0][t][:, 1, :], y_sb[t][:].indirect(n2_t[:, 0:LC]), ACT.Copy)
+            nc.scalar.activation(y_sb[t][:], y_ps[t][:], ACT.Copy, scale=1.0 / 32.0)
+            fetch_y(0, t)
         for t in range(PACK):
-            nc.scalar.activation(d_sb[t][:], d_ps[t][:], ACT.Copy, scale=gain[:, t : t + 1])
-        d_far = [tile([P, HALF], F32, "d_far%d" % t) for t in range(PACK)]
+            leave_d(t)
+            if road(0, t) == "S":
+                fetch_d(0, t)
         for t in range(PACK):
-            nc.scalar.activation(picked[1][t][:, 0, :], y_sb[t][:].indirect(n1_t[:, LC : 2 * LC]), ACT.Copy)
-            nc.scalar.activation(picked[1][t][:, 1, :], y_sb[t][:].indirect(n2_t[:, LC : 2 * LC]), ACT.Copy)
-            nc.scalar.activation(d_far[t][:], d_sb[t][:].indirect(n3_t[:, LC : 2 * LC]), ACT.Copy)
+            fetch_y(1, t)
+            if road(1, t) == "S":
+                fetch_d(1, t)
 
         h_ps = [[], []]
         for u in range(2):
             cols = slice(u * HALF, (u + 1) * HALF)
             near = tile([P, PACK, HALF], F32, "near%d" % u)
-            far = tile([P, PACK, HALF], F32, "far%d" % u)
-            diff = [tile([P, 2, HALF], F32, "diff%d_%d" % (u, t)) for t in range(PACK)]
+            far = tile([P, PACK, HALF], F32, "far%d" % u, "diff_second" if u == 0 else "")
+            if u == 0:
+                first = placed([P, 2, HALF], F32, "diff_first", 0)
+                rest = placed([P, PACK - 1, 2, HALF], F32, "diff_rest", 16384 - 6144)
+                diff = [first[:]] + [rest[:, t] for t in range(PACK - 1)]
+            else:
+                rest = tile([P, PACK, 2, HALF], F32, "diff_second", "diff_second")
+                diff = [rest[:, t] for t in range(PACK)]
 
             def differences(t):
-                nc.vector.tensor_tensor(
-                    diff[t][:], picked[u][t][:], y_ps[t][:, cols].unsqueeze(1).to_broadcast([P, 2, HALF]), ALU.subtract
+                nc.vector.scalar_tensor_tensor(
+                    diff[t], y_ps[t][:, cols].unsqueeze(1).to_broadcast([P, 2, HALF]), -1.0 / 32.0,
+                    picked[u][:, t, 0:2, :], ALU.mult, ALU.add,
                 )
+                if road(u, t) == "V":
+                    fetch_d(u, t)
 
             def products(t):
                 nc.vector.scalar_tensor_tensor(near[:, t, :], diff[t][:, 0, :], 2.0, d_sb[t][:, cols], ALU.mult, ALU.mult)
-                if u == 0:
-                    nc.vector.tensor_tensor(far[:, t, :], d_sb[t][:].indirect(n3_t[:, 0:LC]), diff[t][:, 1, :], ALU.mult)
+                if road(u, t) == "F":
+                    nc.vector.tensor_tensor(far[:, t, :], d_sb[t][:].indirect(n3_t[:, u * LC : (u + 1) * LC]), diff[t][:, 1, :], ALU.mult)
                 else:
-                    nc.vector.tensor_tensor(far[:, t, :], d_far[t][:], diff[t][:, 1, :], ALU.mult)
+                    (nc.vector).tensor_tensor(far[:, t, :], picked[u][:, t, 2, :], diff[t][:, 1, :], ALU.mult)
 
-            if u == 0:
-                for t in range(PACK):
-                    differences(t)
-                for t in range(PACK):
-                    products(t)
-            else:
-                differences(0)
-                for t in range(PACK):
-                    if t + 1 < PACK:
-                        differences(t + 1)
-                    products(t)
+            differences(0)
+            for t in range(PACK):
+                if t + 1 < PACK:
+                    differences(t + 1)
+                products(t)
             z_bf = tile([P, HALF * PACK], BF16, "z_bf%d" % u)
             nc.vector.tensor_tensor(
                 z_bf[:].rearrange("p (c i t) -> p c t i", i=4, t=PACK),
@@ -212,10 +246,10 @@ def tile_picked_twkeyflowbratio_none_po_kernel(
         pb = [tile([P, W], F32, "pb%d" % t) for t in range(PACK)]
         size = [tile([P, W], F32, "size%d" % t) for t in range(PACK)]
         root = [tile([P, W], F32, "root%d" % t) for t in range(PACK)]
-        larger = [tile([P, W], F32, "larger%d" % t) for t in range(PACK)]
+        larger = [tile([P, W], F32, "larger%d" % t, "planes" if t == PACK - 1 else "") for t in range(PACK)]
         part = [tile([P, W], F32, "part%d" % t) for t in range(PACK)]
         o_sb = [tile([P, S], F32, "o_sb%d" % t) for t in range(PACK)]
-        o_pl = tile([P, PACK, S], BF16, "o_pl")
+        o_pl = tile([P, PACK, S], BF16, "o_pl", "planes")
         o_bf = tile([P, S * PACK], BF16, "o_bf")
 
         def fetch(t):

@@ -52,12 +52,10 @@ def tile_picked_twkeyflowbratio_none_po_kernel(
         xs_win = tile([P, T], U8, "xs_win")
         ds_win = tile([P, T], U8, "ds_win")
         w1s_raw = tile([P, S], U8, "w1s_raw", "dealt_d_scales")
-        w2s_raw = tile([P, S], U8, "w2s_raw")
         nc.vector.memset(xs_win[:, : 3 * T // 4].bitcast(I32), 0)
         nc.gpsimd.memset(xs_win[:, 3 * T // 4 :].bitcast(I32), 0)
         nc.gpsimd.memset(w1s_raw[:].bitcast(I32), 0)
         nc.vector.memset(ds_win[:].bitcast(I32), 0)
-        nc.gpsimd.memset(w2s_raw[:].bitcast(I32), 0)
 
         warm = tile([P, 2], F32, "warm")
         nc.vector.memset(warm[:, 0:1], 1.0)
@@ -77,19 +75,18 @@ def tile_picked_twkeyflowbratio_none_po_kernel(
         nc.sync.dma_start(ds_win[0:P:8, :].bitcast(I32), d_scales[0].bitcast(I32))
         nc.sync.dma_start(xw_win[:].bitcast(I32), x_words[0].rearrange("p n r -> p (n r)").bitcast(I32))
         load_scales(nc.sync, w1s_raw, w1_scales)
+        nc.sync.dma_start(w2w_raw[:].bitcast(I32), w2_words[0].bitcast(I32))
         nc.sync.dma_start(dw_win[:].bitcast(I32), d_words[0].rearrange("p n r -> p (n r)").bitcast(I32))
         n1_t = load_list(n1, "n1_t")
         n2_t = load_list(n2, "n2_t")
         nc.sync.dma_start(gn_sb, gn.rearrange("(p t) o -> p (t o)", t=PACK))
         n3_t = load_list(n3, "n3_t")
-        nc.sync.dma_start(w2w_raw[:].bitcast(I32), w2_words[0].bitcast(I32))
-        load_scales(nc.sync, w2s_raw, w2_scales)
         n4_t = load_list(n4, "n4_t")
         n5_t = load_list(n5, "n5_t")
 
-        def deal_weight(engine, words, words_raw, scales_raw, name):
+        def deal_weight(word_engine, engine, words, words_raw, scales_raw, name):
             scales = tile([P, S], U8, name + "s")
-            engine.tensor_copy(
+            word_engine.tensor_copy(
                 words[:].rearrange("p (t m b) -> p t m b", t=PACK, b=2),
                 words_raw[:].rearrange("p (m t b) -> p t m b", t=PACK, b=2),
             )
@@ -111,7 +108,7 @@ def tile_picked_twkeyflowbratio_none_po_kernel(
         dk_w = tile([P, S], U32, "dk_w")
 
         nc.vector.tensor_copy(xq_s[:], xs_win[:].indirect(offs_t[:]))
-        w1w, w1s = deal_weight(nc.gpsimd, tile([P, 2 * S], U8, "w1w"), w1w_raw, w1s_raw, "w1")
+        w1w, w1s = deal_weight(nc.vector, nc.gpsimd, tile([P, 2 * S], U8, "w1w"), w1w_raw, w1s_raw, "w1")
         nc.vector.tensor_copy(x2_s[:], xs_win[:].indirect(two_t[:]))
         nc.vector.tensor_copy(dk_s_raw[:], ds_win[:].indirect(k1_t[:]))
         nc.vector.tensor_copy(
@@ -144,7 +141,10 @@ def tile_picked_twkeyflowbratio_none_po_kernel(
             )
             d_ps.append(bank)
 
-        w2w, w2s = deal_weight(nc.gpsimd, placed([P, 2 * S], U8, "w2w", 4 * S), w2w_raw, w2s_raw, "w2")
+        w2s_raw = tile([P, S], U8, "w2s_raw", "dealt_d_scales")
+        nc.gpsimd.memset(w2s_raw[:].bitcast(I32), 0)
+        load_scales(nc.sync, w2s_raw, w2_scales)
+        w2w, w2s = deal_weight(nc.gpsimd, nc.vector, tile([P, 2 * S], U8, "w2w"), w2w_raw, w2s_raw, "w2")
 
         y_sb = [tile([P, S], F32, "y_sb%d" % t) for t in range(PACK)]
         d_sb = [tile([P, S], F32, "d_sb%d" % t) for t in range(PACK)]
@@ -156,16 +156,24 @@ def tile_picked_twkeyflowbratio_none_po_kernel(
 
         picked = [tile([P, PACK, 3, HALF], F32, "picked0"), placed([P, PACK, 3, HALF], F32, "picked1", 16384)]
 
+        def fused(u, t):
+            return (u == 0 and t < 2) or (u, t) == (1, 0)
+
+        plain_y = tile([P, 2, PACK, HALF], F32, "plain_y")
+
         def road(u, t):
-            return "F" if u == 0 and t < 2 else "S"
+            return "S"
 
         def leave_d(t):
-            if True:
+            if False:
                 nc.vector.tensor_scalar(d_sb[t][:], d_ps[t][:], gn_sb[:, t : t + 1], None, ALU.mult)
             else:
                 nc.scalar.activation(d_sb[t][:], d_ps[t][:], ACT.Copy, scale=gn_sb[:, t : t + 1])
 
         def fetch_y(u, t):
+            if fused(u, t):
+                nc.gpsimd.tensor_copy(plain_y[:, u, t, :], y_sb[t][:, u * HALF : (u + 1) * HALF])
+                return
             nc.scalar.activation(picked[u][:, t, 0, :], y_sb[t][:].indirect(n1_t[:, u * LC : (u + 1) * LC]), ACT.Copy)
             nc.scalar.activation(picked[u][:, t, 1, :], y_sb[t][:].indirect(n2_t[:, u * LC : (u + 1) * LC]), ACT.Copy)
 
@@ -178,11 +186,14 @@ def tile_picked_twkeyflowbratio_none_po_kernel(
 
         for t in range(PACK):
             nc.scalar.activation(y_sb[t][:], y_ps[t][:], ACT.Copy, scale=1.0 / 32.0)
-            fetch_y(0, t)
+            if fused(0, t):
+                fetch_y(0, t)
+        fetch_y(0, 2)
         for t in range(PACK):
             leave_d(t)
-            if road(0, t) == "S":
-                fetch_d(0, t)
+            fetch_d(0, t)
+            if t == 1:
+                fetch_y(0, 3)
         for t in range(PACK):
             fetch_y(1, t)
             if road(1, t) == "S":
@@ -194,14 +205,20 @@ def tile_picked_twkeyflowbratio_none_po_kernel(
             near = tile([P, PACK, HALF], F32, "near%d" % u)
             far = tile([P, PACK, HALF], F32, "far%d" % u, "diff_second" if u == 0 else "")
             if u == 0:
-                first = placed([P, 2, HALF], F32, "diff_first", 0)
-                rest = placed([P, PACK - 1, 2, HALF], F32, "diff_rest", 16384 - 6144)
-                diff = [first[:]] + [rest[:, t] for t in range(PACK - 1)]
+                first = placed([P, 2, HALF], F32, "diff_first", 12288)
+                rest = placed([P, PACK - 1, 2, HALF], F32, "diff_rest", 3072 - 64)
+                diff = [rest[:, t] for t in range(PACK - 1)] + [first[:]]
             else:
                 rest = tile([P, PACK, 2, HALF], F32, "diff_second", "diff_second")
                 diff = [rest[:, t] for t in range(PACK)]
 
             def differences(t):
+                if fused(u, t):
+                    for k, places in enumerate((n1_t, n2_t)):
+                        nc.vector.tensor_tensor(
+                            diff[t][:, k, :], y_sb[t][:].indirect(places[:, u * LC : (u + 1) * LC]), plain_y[:, u, t, :], ALU.subtract
+                        )
+                    return
                 nc.vector.scalar_tensor_tensor(
                     diff[t], y_ps[t][:, cols].unsqueeze(1).to_broadcast([P, 2, HALF]), -1.0 / 32.0,
                     picked[u][:, t, 0:2, :], ALU.mult, ALU.add,
@@ -295,12 +312,17 @@ def tile_picked_twkeyflowbratio_none_po_kernel(
         CUT = 352 // 4
         woven = o_bf[:].rearrange("p (c i t) -> p c t i", i=4, t=PACK)
         planes = o_pl[:].rearrange("p t (c i) -> p c t i", i=4)
-        nc.vector.tensor_copy(woven[:, :CUT], planes[:, :CUT])
+        nc.vector.tensor_copy(woven[:, : HALF // 4], planes[:, : HALF // 4])
+        nc.vector.tensor_copy(woven[:, HALF // 4 : CUT], planes[:, HALF // 4 : CUT])
         nc.scalar.copy(woven[:, CUT:], planes[:, CUT:])
 
         o_w = tile([P, S], U32, "o_w")
         o_s = tile([P, S], U8, "o_s")
-        nc.vector.quantize_mx(o_w[:].bitcast(FP8X4), o_s[:], o_bf[:])
-        nc.sync.dma_start(out_1[0].rearrange("p n r -> p (n r)").bitcast(I32), o_w[:].bitcast(I32))
+        words_out = out_1[0].rearrange("p n r -> p (n r)").bitcast(I32)
+        for u in range(2):
+            cols = slice(u * HALF, (u + 1) * HALF)
+            nc.vector.quantize_mx(o_w[:, cols].bitcast(FP8X4), o_s[:, cols], o_bf[:, u * HALF * PACK : (u + 1) * HALF * PACK])
+            nc.sync.dma_start(words_out[:, cols], o_w[:, cols].bitcast(I32))
         for q in range(4):
-            nc.scalar.dma_start(out_2[0, 4 * q : 4 * q + 4, :].bitcast(I32), o_s[32 * q : 32 * q + 4, :].bitcast(I32))
+            queue = nc.scalar if q < 3 else nc.sync
+            queue.dma_start(out_2[0, 4 * q : 4 * q + 4, :].bitcast(I32), o_s[32 * q : 32 * q + 4, :].bitcast(I32))

@@ -18,7 +18,15 @@ PACK = 4
 S = 512
 T = 2048
 W = 256
-HALF = 256
+LIST_ROWS = 16
+QUADRANTS = 4
+MM_WIDTH = 256
+LINE = 4
+PIECES = ((0, 384), (384, S))
+FUSED_TILES = 2
+ZERO_SPLIT = 3 * T // 4
+ROUND_SPLIT = 320
+Y_SCALE = 1.0 / 32.0
 FLOPS = 3 * 2 * 512 * 512 * 512
 
 
@@ -32,89 +40,82 @@ def tile_picked_twkeyflowbratio_none_po_kernel(
         sb = ctx.enter_context(tc.tile_pool(name="sb", bufs=1))
         psum = ctx.enter_context(tc.psum_pool(name="psum", bufs=1))
 
-        turn = ctx.enter_context(tc.tile_pool(name="turn", bufs=1))
-
         def tile(shape, dtype, name, tag=""):
             return sb.tile(shape, dtype, name=name, tag=tag, align_bytes=64)
 
-        def placed(shape, dtype, name, offset):
-            return turn.tile(shape, dtype, name=name, offset=offset, align_bytes=64)
-
         def load_list(src, name):
-            t = lists.tile(list(src.shape), U16, name=name)
-            nc.sync.dma_start(t[:], src)
-            return t
+            offsets = lists.tile(list(src.shape), U16, name=name)
+            nc.sync.dma_start(offsets[:], src)
+            return offsets
 
-        def load_scales(queue, dst, src):
-            for q in range(4):
-                queue.dma_start(dst[32 * q : 32 * q + 4, :].bitcast(I32), src[0, 4 * q : 4 * q + 4, :].bitcast(I32))
+        def load_scales(dst, src):
+            for q in range(QUADRANTS):
+                nc.sync.dma_start(dst[32 * q : 32 * q + 4, :].bitcast(I32), src[0, 4 * q : 4 * q + 4, :].bitcast(I32))
+
+        def deal(engine, dealt, raw):
+            engine.tensor_copy(dealt[:].rearrange("p (t m) -> p t m", t=PACK), raw[:].rearrange("p (m t) -> p t m", t=PACK))
+
+        def deal_fp4(engine, dealt, raw):
+            engine.tensor_copy(
+                dealt[:].rearrange("p (t m b) -> p t m b", t=PACK, b=2),
+                raw[:].rearrange("p (m t b) -> p t m b", t=PACK, b=2),
+            )
 
         xs_win = tile([P, T], U8, "xs_win")
         ds_win = tile([P, T], U8, "ds_win")
-        w1s_raw = tile([P, S], U8, "w1s_raw", "dealt_d_scales")
-        nc.vector.memset(xs_win[:, : 3 * T // 4].bitcast(I32), 0)
-        nc.gpsimd.memset(xs_win[:, 3 * T // 4 :].bitcast(I32), 0)
+        w1s_raw = tile([P, S], U8, "w1s_raw", "raw_scales")
+        nc.vector.memset(xs_win[:, :ZERO_SPLIT].bitcast(I32), 0)
+        nc.gpsimd.memset(xs_win[:, ZERO_SPLIT:].bitcast(I32), 0)
         nc.gpsimd.memset(w1s_raw[:].bitcast(I32), 0)
         nc.vector.memset(ds_win[:].bitcast(I32), 0)
 
         warm = tile([P, 2], F32, "warm")
         nc.vector.memset(warm[:, 0:1], 1.0)
         nc.scalar.activation(warm[:, 1:2], warm[:, 0:1], ACT.Abs_reciprocal_sqrt)
+
         xw_win = tile([P, T], U32, "xw_win")
         dw_win = tile([P, T], U32, "dw_win")
         w1w_raw = tile([P, 2 * S], U8, "w1w_raw")
         w2w_raw = tile([P, 2 * S], U8, "w2w_raw")
-        gn_wide = placed([P, 32], F32, "gn_wide", 16384 - 64)
-        gn_sb = gn_wide[:, 0:PACK]
+        gn_sb = tile([P, PACK], F32, "gn_sb", "after_gain")
 
-        load_scales(nc.sync, xs_win, x_scales)
+        load_scales(xs_win, x_scales)
         offs_t = load_list(offs, "offs_t")
         two_t = load_list(two, "two_t")
         nc.sync.dma_start(w1w_raw[:].bitcast(I32), w1_words[0].bitcast(I32))
         k1_t = load_list(k1, "k1_t")
         nc.sync.dma_start(ds_win[0:P:8, :].bitcast(I32), d_scales[0].bitcast(I32))
         nc.sync.dma_start(xw_win[:].bitcast(I32), x_words[0].rearrange("p n r -> p (n r)").bitcast(I32))
-        load_scales(nc.sync, w1s_raw, w1_scales)
+        load_scales(w1s_raw, w1_scales)
         nc.sync.dma_start(w2w_raw[:].bitcast(I32), w2_words[0].bitcast(I32))
         nc.sync.dma_start(dw_win[:].bitcast(I32), d_words[0].rearrange("p n r -> p (n r)").bitcast(I32))
         n1_t = load_list(n1, "n1_t")
         n2_t = load_list(n2, "n2_t")
-        nc.sync.dma_start(gn_sb, gn.rearrange("(p t) o -> p (t o)", t=PACK))
+        nc.sync.dma_start(gn_sb[:], gn.rearrange("(p t) o -> p (t o)", t=PACK))
         n3_t = load_list(n3, "n3_t")
         n4_t = load_list(n4, "n4_t")
         n5_t = load_list(n5, "n5_t")
-
-        def deal_weight(word_engine, engine, words, words_raw, scales_raw, name):
-            scales = tile([P, S], U8, name + "s")
-            word_engine.tensor_copy(
-                words[:].rearrange("p (t m b) -> p t m b", t=PACK, b=2),
-                words_raw[:].rearrange("p (m t b) -> p t m b", t=PACK, b=2),
-            )
-            engine.tensor_copy(
-                scales[:].rearrange("p (t m) -> p t m", t=PACK),
-                scales_raw[:].rearrange("p (m t) -> p t m", t=PACK),
-            )
-            return words, scales
 
         xq_s = tile([P, S], U8, "xq_s")
         xq_w = tile([P, S], U32, "xq_w")
         x2_s = tile([P, S], U8, "x2_s")
         dk_s_raw = tile([P, S], U8, "dk_s_raw", "after_d_scales")
         x2_w = tile([P, S], U32, "x2_w", "after_d_scales")
-        dk_w_raw = placed([P, S], U32, "dk_w_raw", 2 * S)
-        dk_s_dealt = tile([P, S], U8, "dk_s_dealt", "dealt_d_scales")
+        dk_w_raw = tile([P, S], U32, "dk_w_raw", "after_d_words")
+        dk_s_dealt = tile([P, S], U8, "dk_s_dealt", "raw_scales")
         dk_s = tile([P, S], U8, "dk_s")
         nc.gpsimd.memset(dk_s[:].bitcast(I32), 0)
         dk_w = tile([P, S], U32, "dk_w")
+        w1w = tile([P, 2 * S], U8, "w1w")
+        w1s = tile([P, S], U8, "w1s")
 
         nc.vector.tensor_copy(xq_s[:], xs_win[:].indirect(offs_t[:]))
-        w1w, w1s = deal_weight(nc.vector, nc.gpsimd, tile([P, 2 * S], U8, "w1w"), w1w_raw, w1s_raw, "w1")
+        deal_fp4(nc.vector, w1w, w1w_raw)
+        deal(nc.gpsimd, w1s, w1s_raw)
         nc.vector.tensor_copy(x2_s[:], xs_win[:].indirect(two_t[:]))
         nc.vector.tensor_copy(dk_s_raw[:], ds_win[:].indirect(k1_t[:]))
-        nc.vector.tensor_copy(
-            dk_s_dealt[:].rearrange("p (t m) -> p t m", t=PACK), dk_s_raw[:].rearrange("p (m t) -> p t m", t=PACK)
-        )
-        for q in range(4):
+        deal(nc.vector, dk_s_dealt, dk_s_raw)
+        for q in range(QUADRANTS):
             nc.sync.dma_start(dk_s[32 * q : 32 * q + 4, :].bitcast(I32), dk_s_dealt[32 * q : 32 * q + 32 : 8, :].bitcast(I32))
         nc.vector.tensor_copy(xq_w[:], xw_win[:].indirect(offs_t[:]))
 
@@ -129,9 +130,7 @@ def tile_picked_twkeyflowbratio_none_po_kernel(
 
         nc.vector.tensor_copy(x2_w[:], xw_win[:].indirect(two_t[:]))
         nc.vector.tensor_copy(dk_w_raw[:], dw_win[:].indirect(k1_t[:]))
-        nc.vector.tensor_copy(
-            dk_w[:].rearrange("p (t m) -> p t m", t=PACK), dk_w_raw[:].rearrange("p (m t) -> p t m", t=PACK)
-        )
+        deal(nc.vector, dk_w, dk_w_raw)
         d_ps = []
         for t in range(PACK):
             bank = psum.tile([P, S], F32, name="d_ps%d" % t, tag="bank_b%d" % t)
@@ -141,188 +140,174 @@ def tile_picked_twkeyflowbratio_none_po_kernel(
             )
             d_ps.append(bank)
 
-        w2s_raw = tile([P, S], U8, "w2s_raw", "dealt_d_scales")
+        w2s_raw = tile([P, S], U8, "w2s_raw", "raw_scales")
         nc.gpsimd.memset(w2s_raw[:].bitcast(I32), 0)
-        load_scales(nc.sync, w2s_raw, w2_scales)
-        w2w, w2s = deal_weight(nc.gpsimd, nc.vector, tile([P, 2 * S], U8, "w2w"), w2w_raw, w2s_raw, "w2")
+        load_scales(w2s_raw, w2_scales)
+        w2w = tile([P, 2 * S], U8, "w2w")
+        w2s = tile([P, S], U8, "w2s")
+        deal_fp4(nc.gpsimd, w2w, w2w_raw)
+        deal(nc.vector, w2s, w2s_raw)
 
         y_sb = [tile([P, S], F32, "y_sb%d" % t) for t in range(PACK)]
         d_sb = [tile([P, S], F32, "d_sb%d" % t) for t in range(PACK)]
         h_sb = [tile([P, S], F32, "h_sb%d" % t) for t in range(PACK)]
-        LC = HALF // 16
+        widths = [end - begin for begin, end in PIECES]
 
-        def on_scalar(u, t):
-            return u == 1
+        def columns(piece):
+            return slice(*PIECES[piece])
 
-        picked = [tile([P, PACK, 3, HALF], F32, "picked0"), placed([P, PACK, 3, HALF], F32, "picked1", 16384)]
+        def entries(offsets, piece):
+            begin, end = PIECES[piece]
+            return offsets[:, begin // LIST_ROWS : end // LIST_ROWS]
 
-        def fused(u, t):
-            return (u == 0 and t < 2) or (u, t) == (1, 0)
+        def fused(piece, t):
+            return piece == 0 and t < FUSED_TILES
 
-        plain_y = tile([P, 2, PACK, HALF], F32, "plain_y")
+        picked = [
+            tile([P, PACK, 3, widths[0]], F32, "picked0"),
+            tile([P, PACK, 3, widths[1]], F32, "picked1", "after_gain"),
+        ]
+        minus_y = [tile([P, widths[0]], F32, "minus_y%d" % t, "after_fused%d" % t) for t in range(FUSED_TILES)]
 
-        def road(u, t):
-            return "S"
-
-        def leave_d(t):
-            if False:
-                nc.vector.tensor_scalar(d_sb[t][:], d_ps[t][:], gn_sb[:, t : t + 1], None, ALU.mult)
+        def fetch_y(piece, t):
+            if fused(piece, t):
+                nc.gpsimd.tensor_scalar(minus_y[t][:], y_sb[t][:, columns(piece)], -1.0, 0.0, ALU.mult, ALU.add)
             else:
-                nc.scalar.activation(d_sb[t][:], d_ps[t][:], ACT.Copy, scale=gn_sb[:, t : t + 1])
+                nc.scalar.activation(picked[piece][:, t, 0, :], y_sb[t][:].indirect(entries(n1_t, piece)), ACT.Copy)
+                nc.scalar.activation(picked[piece][:, t, 1, :], y_sb[t][:].indirect(entries(n2_t, piece)), ACT.Copy)
 
-        def fetch_y(u, t):
-            if fused(u, t):
-                nc.gpsimd.tensor_copy(plain_y[:, u, t, :], y_sb[t][:, u * HALF : (u + 1) * HALF])
-                return
-            nc.scalar.activation(picked[u][:, t, 0, :], y_sb[t][:].indirect(n1_t[:, u * LC : (u + 1) * LC]), ACT.Copy)
-            nc.scalar.activation(picked[u][:, t, 1, :], y_sb[t][:].indirect(n2_t[:, u * LC : (u + 1) * LC]), ACT.Copy)
-
-        def fetch_d(u, t):
-            window = d_sb[t][:].indirect(n3_t[:, u * LC : (u + 1) * LC])
-            if road(u, t) == "S":
-                nc.scalar.activation(picked[u][:, t, 2, :], window, ACT.Copy)
-            if road(u, t) == "V":
-                nc.vector.tensor_copy(picked[u][:, t, 2, :], window)
+        def fetch_d(piece, t):
+            nc.scalar.activation(picked[piece][:, t, 2, :], d_sb[t][:].indirect(entries(n3_t, piece)), ACT.Copy)
 
         for t in range(PACK):
-            nc.scalar.activation(y_sb[t][:], y_ps[t][:], ACT.Copy, scale=1.0 / 32.0)
-            if fused(0, t):
-                fetch_y(0, t)
-        fetch_y(0, 2)
+            nc.scalar.activation(y_sb[t][:], y_ps[t][:], ACT.Copy, scale=Y_SCALE)
         for t in range(PACK):
-            leave_d(t)
+            fetch_y(0, t)
+        for t in range(PACK):
+            nc.scalar.activation(d_sb[t][:], d_ps[t][:], ACT.Copy, scale=gn_sb[:, t : t + 1])
             fetch_d(0, t)
-            if t == 1:
-                fetch_y(0, 3)
         for t in range(PACK):
             fetch_y(1, t)
-            if road(1, t) == "S":
-                fetch_d(1, t)
+            fetch_d(1, t)
 
-        h_ps = [[], []]
-        for u in range(2):
-            cols = slice(u * HALF, (u + 1) * HALF)
-            near = tile([P, PACK, HALF], F32, "near%d" % u)
-            far = tile([P, PACK, HALF], F32, "far%d" % u, "diff_second" if u == 0 else "")
-            if u == 0:
-                first = placed([P, 2, HALF], F32, "diff_first", 12288)
-                rest = placed([P, PACK - 1, 2, HALF], F32, "diff_rest", 3072 - 64)
-                diff = [rest[:, t] for t in range(PACK - 1)] + [first[:]]
+        last_banks = []
+        for piece in range(2):
+            width = widths[piece]
+            cols = columns(piece)
+            near = tile([P, PACK, width], F32, "near%d" % piece)
+            far = tile([P, PACK, width], F32, "far%d" % piece, "after_first_z" if piece == 0 else "")
+            if piece == 0:
+                fused_diffs = tile([P, FUSED_TILES, 2, width], F32, "diff0", "after_d_words")
+                diffs = [fused_diffs[:, t] for t in range(FUSED_TILES)]
             else:
-                rest = tile([P, PACK, 2, HALF], F32, "diff_second", "diff_second")
-                diff = [rest[:, t] for t in range(PACK)]
+                all_diffs = tile([P, PACK, 2, width], F32, "diff1", "after_first_z")
+                diffs = [all_diffs[:, t] for t in range(PACK)]
 
             def differences(t):
-                if fused(u, t):
-                    for k, places in enumerate((n1_t, n2_t)):
+                if fused(piece, t):
+                    for side, offsets in enumerate((n1_t, n2_t)):
                         nc.vector.tensor_tensor(
-                            diff[t][:, k, :], y_sb[t][:].indirect(places[:, u * LC : (u + 1) * LC]), plain_y[:, u, t, :], ALU.subtract
+                            diffs[t][:, side, :], y_sb[t][:].indirect(entries(offsets, piece)), minus_y[t][:], ALU.add
                         )
                     return
+                if piece == 0:
+                    diffs.append(tile([P, 2, width], F32, "diff0_%d" % t, "after_fused%d" % (t - FUSED_TILES))[:])
                 nc.vector.scalar_tensor_tensor(
-                    diff[t], y_ps[t][:, cols].unsqueeze(1).to_broadcast([P, 2, HALF]), -1.0 / 32.0,
-                    picked[u][:, t, 0:2, :], ALU.mult, ALU.add,
+                    diffs[t], y_ps[t][:, cols].unsqueeze(1).to_broadcast([P, 2, width]), -Y_SCALE,
+                    picked[piece][:, t, 0:2, :], ALU.mult, ALU.add,
                 )
-                if road(u, t) == "V":
-                    fetch_d(u, t)
 
             def products(t):
-                nc.vector.scalar_tensor_tensor(near[:, t, :], diff[t][:, 0, :], 2.0, d_sb[t][:, cols], ALU.mult, ALU.mult)
-                if road(u, t) == "F":
-                    nc.vector.tensor_tensor(far[:, t, :], d_sb[t][:].indirect(n3_t[:, u * LC : (u + 1) * LC]), diff[t][:, 1, :], ALU.mult)
-                else:
-                    (nc.vector).tensor_tensor(far[:, t, :], picked[u][:, t, 2, :], diff[t][:, 1, :], ALU.mult)
+                nc.vector.scalar_tensor_tensor(near[:, t, :], diffs[t][:, 0, :], 2.0, d_sb[t][:, cols], ALU.mult, ALU.mult)
+                if piece == 0:
+                    nc.vector.tensor_tensor(far[:, t, :], picked[piece][:, t, 2, :], diffs[t][:, 1, :], ALU.mult)
 
             differences(0)
             for t in range(PACK):
                 if t + 1 < PACK:
                     differences(t + 1)
                 products(t)
-            z_bf = tile([P, HALF * PACK], BF16, "z_bf%d" % u)
+            if piece == 1:
+                nc.vector.tensor_tensor(far[:], picked[piece][:, :, 2, :], all_diffs[:, :, 1, :], ALU.mult)
+            z_bf = tile([P, width * PACK], BF16, "z_bf%d" % piece)
             nc.vector.tensor_tensor(
-                z_bf[:].rearrange("p (c i t) -> p c t i", i=4, t=PACK),
-                near[:].rearrange("p t (c i) -> p c t i", i=4),
-                far[:].rearrange("p t (c i) -> p c t i", i=4),
+                z_bf[:].rearrange("p (c i t) -> p c t i", i=LINE, t=PACK),
+                near[:].rearrange("p t (c i) -> p c t i", i=LINE),
+                far[:].rearrange("p t (c i) -> p c t i", i=LINE),
                 ALU.add,
             )
-            z_w = tile([P, HALF], U32, "z_w%d" % u)
-            z_s = tile([P, HALF], U8, "z_s%d" % u)
+            z_w = tile([P, width], U32, "z_w%d" % piece)
+            z_s = tile([P, width], U8, "z_s%d" % piece)
             nc.vector.quantize_mx(z_w[:].bitcast(FP8X4), z_s[:], z_bf[:])
             for t in range(PACK):
-                bank = psum.tile([P, HALF], F32, name="h_ps%d_%d" % (u, t), tag=("bank_b%d" if u == 0 else "bank_a%d") % t)
-                nc.tensor.matmul_mx(
-                    bank[:], lhsT=w2w[:, 2 * P * t : 2 * P * (t + 1)].bitcast(FP4X4), lhsT_scale=w2s[:, P * t : P * (t + 1)],
-                    rhs=z_w[:].bitcast(FP8X4), rhs_scale=z_s[:], start=True, stop=True,
-                )
-                h_ps[u].append(bank)
-                if u == 0:
+                bank = psum.tile([P, width], F32, name="h_ps%d_%d" % (piece, t), tag=("bank_b%d" if piece == 0 else "bank_a%d") % t)
+                for begin in range(0, width, MM_WIDTH):
+                    run = slice(begin, min(begin + MM_WIDTH, width))
+                    nc.tensor.matmul_mx(
+                        bank[:, run], lhsT=w2w[:, 2 * P * t : 2 * P * (t + 1)].bitcast(FP4X4), lhsT_scale=w2s[:, P * t : P * (t + 1)],
+                        rhs=z_w[:, run].bitcast(FP8X4), rhs_scale=z_s[:, run], start=True, stop=True,
+                    )
+                if piece == 0:
                     nc.scalar.activation(h_sb[t][:, cols], bank[:], ACT.Copy)
+                else:
+                    last_banks.append(bank)
 
         out_rows = out_0.rearrange("(p t) j -> p t j", t=PACK)
-        pa = [tile([P, W], F32, "pa%d" % t) for t in range(PACK)]
-        pb = [tile([P, W], F32, "pb%d" % t) for t in range(PACK)]
-        size = [tile([P, W], F32, "size%d" % t) for t in range(PACK)]
-        root = [tile([P, W], F32, "root%d" % t) for t in range(PACK)]
-        larger = [tile([P, W], F32, "larger%d" % t, "planes" if t == PACK - 1 else "") for t in range(PACK)]
-        part = [tile([P, W], F32, "part%d" % t) for t in range(PACK)]
+        pa = [tile([P, 2, W], F32, "pa%d" % e) for e in range(2)]
+        pb = [tile([P, 2, W], F32, "pb%d" % e) for e in range(2)]
+        size = [tile([P, 2, W], F32, "size%d" % e) for e in range(2)]
+        root = [tile([P, 2, W], F32, "root%d" % e) for e in range(2)]
+        larger = [tile([P, 2, W], F32, "larger%d" % e) for e in range(2)]
+        part = [tile([P, 2, W], F32, "part%d" % e) for e in range(2)]
         o_sb = [tile([P, S], F32, "o_sb%d" % t) for t in range(PACK)]
-        o_pl = tile([P, PACK, S], BF16, "o_pl", "planes")
         o_bf = tile([P, S * PACK], BF16, "o_bf")
 
-        def fetch(t):
-            if t == 2:
-                nc.vector.tensor_copy(h_sb[t][:, HALF:], h_ps[1][t][:])
+        for t in range(PACK):
+            nc.scalar.activation(h_sb[t][:, columns(1)], last_banks[t][:], ACT.Copy)
+
+        for e in range(2):
+            for r in range(2):
+                nc.vector.tensor_copy(pb[e][:, r, :], h_sb[2 * e + r][:].indirect(n5_t[:]))
+                nc.scalar.activation(pa[e][:, r, :], h_sb[2 * e + r][:].indirect(n4_t[:]), ACT.Copy)
+            if e == 0:
+                nc.vector.scalar_tensor_tensor(size[e][:], pb[e][:], -1.0, pb[e][:], ALU.mult, ALU.max)
             else:
-                nc.scalar.activation(h_sb[t][:, HALF:], h_ps[1][t][:], ACT.Copy)
-            nc.scalar.activation(pa[t][:], h_sb[t][:].indirect(n4_t[:]), ACT.Copy)
-            nc.vector.tensor_copy(pb[t][:], h_sb[t][:].indirect(n5_t[:]))
+                nc.scalar.activation(size[e][:], pb[e][:], ACT.Abs)
+            nc.scalar.activation(root[e][:], size[e][:], ACT.Abs_reciprocal_sqrt, bias=0.5)
+            nc.vector.tensor_tensor(larger[e][:], pa[e][:], pb[e][:], ALU.max)
+            nc.vector.tensor_tensor(part[e][:], pa[e][:], root[e][:], ALU.mult)
 
-        def combine(t):
-            nc.vector.scalar_tensor_tensor(size[t][:], pb[t][:], -1.0, pb[t][:], ALU.mult, ALU.max)
-            nc.vector.tensor_tensor(larger[t][:], pa[t][:], pb[t][:], ALU.max)
+        def put_larger(e, r):
+            nc.scalar.activation(o_sb[2 * e + r][:].indirect(n5_t[:]), larger[e][:, r, :], ACT.Copy)
 
-        def put_larger(t):
-            nc.scalar.activation(root[t][:], size[t][:], ACT.Abs_reciprocal_sqrt, bias=0.5)
-            nc.scalar.activation(o_sb[t][:].indirect(n5_t[:]), larger[t][:], ACT.Copy)
-            nc.vector.tensor_tensor(part[t][:], pa[t][:], root[t][:], ALU.mult)
+        def put_ratio(e, r):
+            nc.vector.tensor_tensor(o_sb[2 * e + r][:].indirect(n4_t[:]), part[e][:, r, :], root[e][:, r, :], ALU.mult)
 
-        def put_ratio(t):
-            nc.vector.tensor_tensor(o_sb[t][:].indirect(n4_t[:]), part[t][:], root[t][:], ALU.mult)
-            nc.sync.dma_start(out_rows[:, t, :], o_sb[t][:])
+        for e in range(2):
+            put_larger(e, 0)
+            put_ratio(e, 1)
+            put_ratio(e, 0)
+            put_larger(e, 1)
+            for r in range(2):
+                nc.sync.dma_start(out_rows[:, 2 * e + r, :], o_sb[2 * e + r][:])
 
-        fetch(0)
-        combine(0)
-        fetch(1)
-        combine(1)
-        put_larger(0)
-        fetch(2)
-        put_ratio(0)
-        combine(2)
-        put_larger(1)
-        put_ratio(1)
-        fetch(3)
-        combine(3)
-        put_larger(2)
-        put_ratio(2)
-        put_larger(3)
-        put_ratio(3)
-        for t in range(PACK - 1):
-            nc.scalar.activation(o_pl[:, t, :], o_sb[t][:], ACT.Copy)
-        nc.vector.tensor_copy(o_pl[:, PACK - 1, :], o_sb[PACK - 1][:])
-        CUT = 352 // 4
-        woven = o_bf[:].rearrange("p (c i t) -> p c t i", i=4, t=PACK)
-        planes = o_pl[:].rearrange("p t (c i) -> p c t i", i=4)
-        nc.vector.tensor_copy(woven[:, : HALF // 4], planes[:, : HALF // 4])
-        nc.vector.tensor_copy(woven[:, HALF // 4 : CUT], planes[:, HALF // 4 : CUT])
-        nc.scalar.copy(woven[:, CUT:], planes[:, CUT:])
+        pairs = tile([P, 2, S, 2], BF16, "pairs")
+        for t in range(PACK):
+            nc.vector.tensor_copy(pairs[:, t // 2, :ROUND_SPLIT, t % 2], o_sb[t][:, :ROUND_SPLIT])
+            nc.scalar.activation(pairs[:, t // 2, ROUND_SPLIT:, t % 2], o_sb[t][:, ROUND_SPLIT:], ACT.Copy)
+        woven = o_bf[:].bitcast(F32).rearrange("p (c i e) -> p c e i", i=LINE, e=2)
+        words = pairs[:].rearrange("p e c r -> p e (c r)").bitcast(F32).rearrange("p e (c i) -> p c e i", i=LINE)
+        half = S // 2
+        nc.vector.tensor_copy(woven[:, : half // LINE], words[:, : half // LINE])
+        nc.scalar.copy(woven[:, half // LINE :], words[:, half // LINE :])
 
         o_w = tile([P, S], U32, "o_w")
         o_s = tile([P, S], U8, "o_s")
         words_out = out_1[0].rearrange("p n r -> p (n r)").bitcast(I32)
-        for u in range(2):
-            cols = slice(u * HALF, (u + 1) * HALF)
-            nc.vector.quantize_mx(o_w[:, cols].bitcast(FP8X4), o_s[:, cols], o_bf[:, u * HALF * PACK : (u + 1) * HALF * PACK])
-            nc.sync.dma_start(words_out[:, cols], o_w[:, cols].bitcast(I32))
-        for q in range(4):
-            queue = nc.scalar if q < 3 else nc.sync
+        for begin in range(0, S, half):
+            span = slice(begin, begin + half)
+            nc.vector.quantize_mx(o_w[:, span].bitcast(FP8X4), o_s[:, span], o_bf[:, begin * PACK : (begin + half) * PACK])
+            nc.sync.dma_start(words_out[:, span], o_w[:, span].bitcast(I32))
+        for q in range(QUADRANTS):
+            queue = nc.scalar if q < QUADRANTS - 1 else nc.sync
             queue.dma_start(out_2[0, 4 * q : 4 * q + 4, :].bitcast(I32), o_s[32 * q : 32 * q + 4, :].bitcast(I32))

from contextlib import ExitStack

import concourse.mybir as mybir

F32 = mybir.dt.float32
BF16 = mybir.dt.bfloat16
I32 = mybir.dt.int32
U32 = mybir.dt.uint32
U16 = mybir.dt.uint16
U8 = mybir.dt.uint8
FP8X4 = mybir.dt.float8_e4m3fn_x4
FP4X4 = mybir.dt.float4_e2m1fn_x4
ALU = mybir.AluOpType
ACT = mybir.ActivationFunctionType

P = 128
PACK = 4
S = 512
T = 2048
W = 256
LIST_ROWS = 16
QUADRANTS = 4
MM_WIDTH = 256
LINE = 4
PIECES = ((0, 384), (384, S))
FUSED_TILES = 2
ZERO_SPLIT = 3 * T // 4
ROUND_SPLIT = 320
Y_SCALE = 1.0 / 32.0
FLOPS = 3 * 2 * 512 * 512 * 512


def tile_picked_twkeyflowbratio_none_po_kernel(
    tc, x_words, x_scales, w1_words, w1_scales, d_words, d_scales, gn, w2_words, w2_scales,
    offs, k1, two, n1, n2, n3, n4, n5, out_0, out_1, out_2,
):
    nc = tc.nc
    with ExitStack() as ctx:
        lists = ctx.enter_context(tc.tile_pool(name="lists", bufs=1))
        sb = ctx.enter_context(tc.tile_pool(name="sb", bufs=1))
        psum = ctx.enter_context(tc.psum_pool(name="psum", bufs=1))

        def tile(shape, dtype, name, tag=""):
            return sb.tile(shape, dtype, name=name, tag=tag, align_bytes=64)

        def load_list(src, name):
            offsets = lists.tile(list(src.shape), U16, name=name)
            nc.sync.dma_start(offsets[:], src)
            return offsets

        def load_scales(dst, src):
            for q in range(QUADRANTS):
                nc.sync.dma_start(dst[32 * q : 32 * q + 4, :].bitcast(I32), src[0, 4 * q : 4 * q + 4, :].bitcast(I32))

        def deal(engine, dealt, raw):
            engine.tensor_copy(dealt[:].rearrange("p (t m) -> p t m", t=PACK), raw[:].rearrange("p (m t) -> p t m", t=PACK))

        def deal_fp4(engine, dealt, raw):
            engine.tensor_copy(
                dealt[:].rearrange("p (t m b) -> p t m b", t=PACK, b=2),
                raw[:].rearrange("p (m t b) -> p t m b", t=PACK, b=2),
            )

        xs_win = tile([P, T], U8, "xs_win")
        ds_win = tile([P, T], U8, "ds_win")
        w1s_raw = tile([P, S], U8, "w1s_raw", "raw_scales")
        nc.vector.memset(xs_win[:, :ZERO_SPLIT].bitcast(I32), 0)
        nc.gpsimd.memset(xs_win[:, ZERO_SPLIT:].bitcast(I32), 0)
        nc.gpsimd.memset(w1s_raw[:].bitcast(I32), 0)
        nc.vector.memset(ds_win[:].bitcast(I32), 0)

        warm = tile([P, 2], F32, "warm")
        nc.vector.memset(warm[:, 0:1], 1.0)
        nc.scalar.activation(warm[:, 1:2], warm[:, 0:1], ACT.Abs_reciprocal_sqrt)

        xw_win = tile([P, T], U32, "xw_win")
        dw_win = tile([P, T], U32, "dw_win")
        w1w_raw = tile([P, 2 * S], U8, "w1w_raw")
        w2w_raw = tile([P, 2 * S], U8, "w2w_raw")
        gn_sb = tile([P, PACK], F32, "gn_sb", "after_gain")

        load_scales(xs_win, x_scales)
        offs_t = load_list(offs, "offs_t")
        two_t = load_list(two, "two_t")
        nc.sync.dma_start(w1w_raw[:].bitcast(I32), w1_words[0].bitcast(I32))
        k1_t = load_list(k1, "k1_t")
        nc.sync.dma_start(ds_win[0:P:8, :].bitcast(I32), d_scales[0].bitcast(I32))
        nc.sync.dma_start(xw_win[:].bitcast(I32), x_words[0].rearrange("p n r -> p (n r)").bitcast(I32))
        load_scales(w1s_raw, w1_scales)
        nc.sync.dma_start(w2w_raw[:].bitcast(I32), w2_words[0].bitcast(I32))
        nc.sync.dma_start(dw_win[:].bitcast(I32), d_words[0].rearrange("p n r -> p (n r)").bitcast(I32))
        n1_t = load_list(n1, "n1_t")
        n2_t = load_list(n2, "n2_t")
        nc.sync.dma_start(gn_sb[:], gn.rearrange("(p t) o -> p (t o)", t=PACK))
        n3_t = load_list(n3, "n3_t")
        n4_t = load_list(n4, "n4_t")
        n5_t = load_list(n5, "n5_t")

        xq_s = tile([P, S], U8, "xq_s")
        xq_w = tile([P, S], U32, "xq_w")
        x2_s = tile([P, S], U8, "x2_s")
        dk_s_raw = tile([P, S], U8, "dk_s_raw", "after_d_scales")
        x2_w = tile([P, S], U32, "x2_w", "after_d_scales")
        dk_w_raw = tile([P, S], U32, "dk_w_raw", "after_d_words")
        dk_s_dealt = tile([P, S], U8, "dk_s_dealt", "raw_scales")
        dk_s = tile([P, S], U8, "dk_s")
        nc.gpsimd.memset(dk_s[:].bitcast(I32), 0)
        dk_w = tile([P, S], U32, "dk_w")
        w1w = tile([P, 2 * S], U8, "w1w")
        w1s = tile([P, S], U8, "w1s")

        nc.vector.tensor_copy(xq_s[:], xs_win[:].indirect(offs_t[:]))
        deal_fp4(nc.vector, w1w, w1w_raw)
        deal(nc.gpsimd, w1s, w1s_raw)
        nc.vector.tensor_copy(x2_s[:], xs_win[:].indirect(two_t[:]))
        nc.vector.tensor_copy(dk_s_raw[:], ds_win[:].indirect(k1_t[:]))
        deal(nc.vector, dk_s_dealt, dk_s_raw)
        for q in range(QUADRANTS):
            nc.sync.dma_start(dk_s[32 * q : 32 * q + 4, :].bitcast(I32), dk_s_dealt[32 * q : 32 * q + 32 : 8, :].bitcast(I32))
        nc.vector.tensor_copy(xq_w[:], xw_win[:].indirect(offs_t[:]))

        y_ps = []
        for t in range(PACK):
            bank = psum.tile([P, S], F32, name="y_ps%d" % t, tag="bank_a%d" % t)
            nc.tensor.matmul_mx(
                bank[:], lhsT=w1w[:, 2 * P * t : 2 * P * (t + 1)].bitcast(FP4X4), lhsT_scale=w1s[:, P * t : P * (t + 1)],
                rhs=xq_w[:].bitcast(FP8X4), rhs_scale=xq_s[:], start=True, stop=True,
            )
            y_ps.append(bank)

        nc.vector.tensor_copy(x2_w[:], xw_win[:].indirect(two_t[:]))
        nc.vector.tensor_copy(dk_w_raw[:], dw_win[:].indirect(k1_t[:]))
        deal(nc.vector, dk_w, dk_w_raw)
        d_ps = []
        for t in range(PACK):
            bank = psum.tile([P, S], F32, name="d_ps%d" % t, tag="bank_b%d" % t)
            nc.tensor.matmul_mx(
                bank[:], lhsT=dk_w[:, P * t : P * (t + 1)].bitcast(FP8X4), lhsT_scale=dk_s[:, P * t : P * (t + 1)],
                rhs=x2_w[:].bitcast(FP8X4), rhs_scale=x2_s[:], start=True, stop=True,
            )
            d_ps.append(bank)

        w2s_raw = tile([P, S], U8, "w2s_raw", "raw_scales")
        nc.gpsimd.memset(w2s_raw[:].bitcast(I32), 0)
        load_scales(w2s_raw, w2_scales)
        w2w = tile([P, 2 * S], U8, "w2w")
        w2s = tile([P, S], U8, "w2s")
        deal_fp4(nc.gpsimd, w2w, w2w_raw)
        deal(nc.vector, w2s, w2s_raw)

        y_sb = [tile([P, S], F32, "y_sb%d" % t) for t in range(PACK)]
        d_sb = [tile([P, S], F32, "d_sb%d" % t) for t in range(PACK)]
        h_sb = [tile([P, S], F32, "h_sb%d" % t) for t in range(PACK)]
        widths = [end - begin for begin, end in PIECES]

        def columns(piece):
            return slice(*PIECES[piece])

        def entries(offsets, piece):
            begin, end = PIECES[piece]
            return offsets[:, begin // LIST_ROWS : end // LIST_ROWS]

        def fused(piece, t):
            return piece == 0 and t < FUSED_TILES

        picked = [
            tile([P, PACK, 3, widths[0]], F32, "picked0"),
            tile([P, PACK, 3, widths[1]], F32, "picked1", "after_gain"),
        ]
        minus_y = [tile([P, widths[0]], F32, "minus_y%d" % t, "after_fused%d" % t) for t in range(FUSED_TILES)]

        def fetch_y(piece, t):
            if fused(piece, t):
                nc.gpsimd.tensor_scalar(minus_y[t][:], y_sb[t][:, columns(piece)], -1.0, 0.0, ALU.mult, ALU.add)
            else:
                nc.scalar.activation(picked[piece][:, t, 0, :], y_sb[t][:].indirect(entries(n1_t, piece)), ACT.Copy)
                nc.scalar.activation(picked[piece][:, t, 1, :], y_sb[t][:].indirect(entries(n2_t, piece)), ACT.Copy)

        def fetch_d(piece, t):
            nc.scalar.activation(picked[piece][:, t, 2, :], d_sb[t][:].indirect(entries(n3_t, piece)), ACT.Copy)

        for t in range(PACK):
            nc.scalar.activation(y_sb[t][:], y_ps[t][:], ACT.Copy, scale=Y_SCALE)
        for t in range(PACK):
            fetch_y(0, t)
        for t in range(PACK):
            nc.scalar.activation(d_sb[t][:], d_ps[t][:], ACT.Copy, scale=gn_sb[:, t : t + 1])
            fetch_d(0, t)
        for t in range(PACK):
            fetch_y(1, t)
            fetch_d(1, t)

        last_banks = []
        for piece in range(2):
            width = widths[piece]
            cols = columns(piece)
            near = tile([P, PACK, width], F32, "near%d" % piece)
            far = tile([P, PACK, width], F32, "far%d" % piece, "after_first_z" if piece == 0 else "")
            if piece == 0:
                fused_diffs = tile([P, FUSED_TILES, 2, width], F32, "diff0", "after_d_words")
                diffs = [fused_diffs[:, t] for t in range(FUSED_TILES)]
            else:
                all_diffs = tile([P, PACK, 2, width], F32, "diff1", "after_first_z")
                diffs = [all_diffs[:, t] for t in range(PACK)]

            def differences(t):
                if fused(piece, t):
                    for side, offsets in enumerate((n1_t, n2_t)):
                        nc.vector.tensor_tensor(
                            diffs[t][:, side, :], y_sb[t][:].indirect(entries(offsets, piece)), minus_y[t][:], ALU.add
                        )
                    return
                if piece == 0:
                    diffs.append(tile([P, 2, width], F32, "diff0_%d" % t, "after_fused%d" % (t - FUSED_TILES))[:])
                nc.vector.scalar_tensor_tensor(
                    diffs[t], y_ps[t][:, cols].unsqueeze(1).to_broadcast([P, 2, width]), -Y_SCALE,
                    picked[piece][:, t, 0:2, :], ALU.mult, ALU.add,
                )

            def products(t):
                nc.vector.scalar_tensor_tensor(near[:, t, :], diffs[t][:, 0, :], 2.0, d_sb[t][:, cols], ALU.mult, ALU.mult)
                if piece == 0:
                    nc.vector.tensor_tensor(far[:, t, :], picked[piece][:, t, 2, :], diffs[t][:, 1, :], ALU.mult)

            differences(0)
            for t in range(PACK):
                if t + 1 < PACK:
                    differences(t + 1)
                products(t)
            if piece == 1:
                nc.vector.tensor_tensor(far[:], picked[piece][:, :, 2, :], all_diffs[:, :, 1, :], ALU.mult)
            z_bf = tile([P, width * PACK], BF16, "z_bf%d" % piece)
            nc.vector.tensor_tensor(
                z_bf[:].rearrange("p (c i t) -> p c t i", i=LINE, t=PACK),
                near[:].rearrange("p t (c i) -> p c t i", i=LINE),
                far[:].rearrange("p t (c i) -> p c t i", i=LINE),
                ALU.add,
            )
            z_w = tile([P, width], U32, "z_w%d" % piece)
            z_s = tile([P, width], U8, "z_s%d" % piece)
            nc.vector.quantize_mx(z_w[:].bitcast(FP8X4), z_s[:], z_bf[:])
            for t in range(PACK):
                bank = psum.tile([P, width], F32, name="h_ps%d_%d" % (piece, t), tag=("bank_b%d" if piece == 0 else "bank_a%d") % t)
                for begin in range(0, width, MM_WIDTH):
                    run = slice(begin, min(begin + MM_WIDTH, width))
                    nc.tensor.matmul_mx(
                        bank[:, run], lhsT=w2w[:, 2 * P * t : 2 * P * (t + 1)].bitcast(FP4X4), lhsT_scale=w2s[:, P * t : P * (t + 1)],
                        rhs=z_w[:, run].bitcast(FP8X4), rhs_scale=z_s[:, run], start=True, stop=True,
                    )
                if piece == 0:
                    nc.scalar.activation(h_sb[t][:, cols], bank[:], ACT.Copy)
                else:
                    last_banks.append(bank)

        out_rows = out_0.rearrange("(p t) j -> p t j", t=PACK)
        pa = [tile([P, 2, W], F32, "pa%d" % e) for e in range(2)]
        pb = [tile([P, 2, W], F32, "pb%d" % e) for e in range(2)]
        size = [tile([P, 2, W], F32, "size%d" % e) for e in range(2)]
        root = [tile([P, 2, W], F32, "root%d" % e) for e in range(2)]
        larger = [tile([P, 2, W], F32, "larger%d" % e) for e in range(2)]
        part = [tile([P, 2, W], F32, "part%d" % e) for e in range(2)]
        o_sb = [tile([P, S], F32, "o_sb%d" % t) for t in range(PACK)]
        o_bf = tile([P, S * PACK], BF16, "o_bf")

        for t in range(PACK):
            nc.scalar.activation(h_sb[t][:, columns(1)], last_banks[t][:], ACT.Copy)

        for e in range(2):
            for r in range(2):
                nc.vector.tensor_copy(pb[e][:, r, :], h_sb[2 * e + r][:].indirect(n5_t[:]))
                nc.scalar.activation(pa[e][:, r, :], h_sb[2 * e + r][:].indirect(n4_t[:]), ACT.Copy)
            if e == 0:
                nc.vector.scalar_tensor_tensor(size[e][:], pb[e][:], -1.0, pb[e][:], ALU.mult, ALU.max)
            else:
                nc.scalar.activation(size[e][:], pb[e][:], ACT.Abs)
            nc.scalar.activation(root[e][:], size[e][:], ACT.Abs_reciprocal_sqrt, bias=0.5)
            nc.vector.tensor_tensor(larger[e][:], pa[e][:], pb[e][:], ALU.max)
            nc.vector.tensor_tensor(part[e][:], pa[e][:], root[e][:], ALU.mult)

        def put_larger(e, r):
            nc.scalar.activation(o_sb[2 * e + r][:].indirect(n5_t[:]), larger[e][:, r, :], ACT.Copy)

        def put_ratio(e, r):
            nc.vector.tensor_tensor(o_sb[2 * e + r][:].indirect(n4_t[:]), part[e][:, r, :], root[e][:, r, :], ALU.mult)

        for e in range(2):
            put_larger(e, 0)
            put_ratio(e, 1)
            put_ratio(e, 0)
            put_larger(e, 1)
            for r in range(2):
                nc.sync.dma_start(out_rows[:, 2 * e + r, :], o_sb[2 * e + r][:])

        pairs = tile([P, 2, S, 2], BF16, "pairs")
        for t in range(PACK):
            nc.vector.tensor_copy(pairs[:, t // 2, :ROUND_SPLIT, t % 2], o_sb[t][:, :ROUND_SPLIT])
            nc.scalar.activation(pairs[:, t // 2, ROUND_SPLIT:, t % 2], o_sb[t][:, ROUND_SPLIT:], ACT.Copy)
        woven = o_bf[:].bitcast(F32).rearrange("p (c i e) -> p c e i", i=LINE, e=2)
        words = pairs[:].rearrange("p e c r -> p e (c r)").bitcast(F32).rearrange("p e (c i) -> p c e i", i=LINE)
        half = S // 2
        nc.vector.tensor_copy(woven[:, : half // LINE], words[:, : half // LINE])
        nc.scalar.copy(woven[:, half // LINE :], words[:, half // LINE :])

        o_w = tile([P, S], U32, "o_w")
        o_s = tile([P, S], U8, "o_s")
        words_out = out_1[0].rearrange("p n r -> p (n r)").bitcast(I32)
        for begin in range(0, S, half):
            span = slice(begin, begin + half)
            nc.vector.quantize_mx(o_w[:, span].bitcast(FP8X4), o_s[:, span], o_bf[:, begin * PACK : (begin + half) * PACK])
            nc.sync.dma_start(words_out[:, span], o_w[:, span].bitcast(I32))
        for q in range(QUADRANTS):
            queue = nc.scalar if q < QUADRANTS - 1 else nc.sync
            queue.dma_start(out_2[0, 4 * q : 4 * q + 4, :].bitcast(I32), o_s[32 * q : 32 * q + 4, :].bitcast(I32))
